import numpy as np, ml_dtypes
CORES = [6,15,38,47]
N = 4
BF = ml_dtypes.bfloat16
W, L, P, ST, IP = 4096, 128, 16, 6, 0.0625
def probes(s, w):
    u = np.sum(w[:, :, 0:1] * s, axis=1); v = 2 * (np.sum(w[:, :, 1:2] * s, axis=1) & (W // 2 - 1)) + 1
    return (u[:, None, :] + np.arange(P)[None, :, None] * v[:, None, :]) & (W - 1)
def margins(rng, share):
    k = (N, 8, 1, W)
    return np.where(rng.random(k) < share, 0.03 * rng.random(k), 0.1 + 0.4 * rng.random(k))
def sizes(rng):
    return rng.choice(np.array([0, 2, 6, 20]), (N, 8, 1, W))
def rules(rng, z, m):
    h = (N, 8, 16, W); m = m.astype(np.float32); z = np.minimum(z, 0.5).astype(np.float32)
    e = (np.minimum(np.floor((2 * m + 1) * rng.random(h, dtype=np.float32)), 2 * m) - m).astype(np.int32)
    a = np.maximum(0, -e); b = 255 - np.maximum(0, e)
    lo = a + np.floor(z * rng.random(h, dtype=np.float32) * (b - a)).astype(np.int32)
    hi = b - np.floor(z * rng.random(h, dtype=np.float32) * (b - a)).astype(np.int32)
    return lo, hi, e
def start(rng):
    s = rng.integers(0, 256, (N, 8, 16, L)); s = np.where(rng.random((N, 8, 1, L)) < 0.5, s, 64 + s // 2)
    return s, rng.integers(0, 2048, (N, 8, 16, 2)), rng.integers(0, 256, (N, 8, 16, ST)) >> rng.integers(0, 4, (N, 8, 16, ST))
def put(lo, hi, e, q, g, c, a, b, f):
    c, k = np.unique(c, return_index=True)
    lo[q, g][:, c] = a[:, k]; hi[q, g][:, c] = b[:, k]; e[q, g][:, c] = f[:, k]
def pack(lo, hi, e, s, w, d):
    t = lambda x: np.ascontiguousarray(x.reshape(N, 128, -1)).astype(np.float32).astype(BF)
    return {"lo": t(lo), "hi": t(hi), "ef": t(e), "s0": t(s), "wt": np.ascontiguousarray(w.reshape(N, 128, 2)).astype(np.int32), "dr": t(d)}
def setup_inputs(rng):
    share = rng.choice(np.array([1.5, 2.5, 4.0, 6.0]), (N, 8, 1, 1)) * IP
    return pack(*rules(rng, margins(rng, share), sizes(rng)), *start(rng))
def setup_inputs_alike(rng):
    z = margins(rng, 3 * IP); z[:, ::2] = 0.1
    lo, hi, e = rules(rng, z, sizes(rng)); s, w, d = start(rng)
    w[:, 0] = 0; w[:, 4] = 0; w[:, 2] = 0; w[:, 2, 0, 0] = 1; w[:, 6] = 0; w[:, 6, 15, 1] = W // 2 - 1; s[:, 6, 15] = 1
    k = rng.integers(0, 5, (N, 4, 1, L)); s[:, 1::2] = np.take_along_axis(s[:, 1::2, :, :5], k, 3)
    s[:, 5] = 255; s[:, 5, 15] = 255 - rng.integers(0, 4, (N, L)); s[:, 5, 15, :4] = 255 - np.arange(4)
    w[:, 5, :, 0] = 2047; w[:, 5, :, 1] = 0; w[:, 5, 0, 1] = 257
    x = np.full((8, 16, 4), 255); x[:, 15] = 255 - np.arange(4); b = x[5]
    for q in range(N):
        c = probes(x, w[q])[5]; a = rng.integers(0, 200, (16, 4 * P))
        put(lo, hi, e, q, 5, c.reshape(-1), a, a, 0 * a)
        a = b - rng.integers(0, 10, (16, 4)); a[15] = b[15]
        m = np.zeros((16, 4), np.int64); m[15] = np.arange(4) - rng.permutation(4)
        put(lo, hi, e, q, 5, c[P - 1], a, b, m)
    return pack(lo, hi, e, s, w, d)
def setup_inputs_chains(rng):
    lo, hi, e = rules(rng, margins(rng, 0.5 * IP), sizes(rng)); s, w, d = start(rng)
    s[:, ::2] = rng.choice(np.array([0, 1, 254, 255]), (N, 4, 16, L)); s[:, 2:4, :, 0] = 0
    for q in range(N):
        c = probes(s[q], w[q]); k = rng.choice(np.array([0, 1, 2, P // 2, P - 1]), (8, L)); k[2:4, 0] = 2
        for g in range(8): put(lo, hi, e, q, g, c[g, k[g], np.arange(L)], s[q, g], s[q, g], s[(q + 1) % N, g] - s[q, g])
    lo[:, 2:4, :, :2] = 1; hi[:, 2:4, :, :2] = 1; e[:, 2:4, :, :2] = 0
    d[:, 0] = 0; d[:, 1] = 255
    return pack(lo, hi, e, s, w, d)
def setup_inputs_full(rng):
    lo = rng.integers(0, 256, (N, 8, 16, W)); hi = lo.copy(); e = rng.integers(0, 256, (N, 8, 16, W)) - lo
    s, w, d = start(rng); s = rng.integers(100, 156, (N, 8, 16, L)); w = np.zeros((N, 8, 16, 2), np.int64); M = W // L; j = np.arange(L)
    for g in range(8):
        val = np.concatenate([rng.permutation(255)[:L - 1], np.array([255])]) if g % 2 == 0 else np.arange(L)
        for q in range(N):
            s[q, g, 0] = rng.permutation(val)
            if g % 2 == 0:
                s[q, g, 1] = 2; w[q, g, 0, 0] = 1; w[q, g, 1, 0] = 128 * (rng.integers(0, W // 256) if g < 6 else W // 256 - 1)
                k = np.full(L, rng.integers(0, 2))
            else:
                s[q, g, 1] = 1; w[q, g, 0, 0] = M; w[q, g, 1, 0] = rng.integers(0, M) if g < 7 else M - 1
                k = rng.integers(0, 2, L)
            w[q, g, 1, 1] = rng.integers(0, 2048)
            c = probes(s[q], w[q])[g]
            a = rng.integers(10, 65, (16, L)); b = rng.integers(191, 246, (16, L)); m = rng.integers(-9, 10, (16, L)); m[15] = rng.integers(1, 10, L)
            a[0] = s[q, g, 0]; b[0] = s[q, g, 0]; m[0] = rng.permutation(val) - s[q, g, 0]; a[1] = 0; b[1] = 255; m[1] = 0
            put(lo, hi, e, q, g, c[k, j], a, b, m)
    return pack(lo, hi, e, s, w, d)
def setup_inputs_ties(rng):
    lo, hi, e = rules(rng, margins(rng, 2.5 * IP), sizes(rng)); s, w, d = start(rng)
    for q in range(N):
        c = probes(s[q], w[q]); o = rng.permutation(8)
        for g in o[:2]:
            lo[q, g] = rng.integers(0, 256, (16, W)); hi[q, g] = lo[q, g]; e[q, g] = rng.integers(0, 256, (16, W)) - lo[q, g]
        for g in o[2:4]:
            lo[q, g] = 0; hi[q, g] = 255; e[q, g] = 0
        for g in o[4:]:
            x = s[q, g]; mode = rng.integers(0, 4, (1, L)); k = rng.integers(0, 3, L)
            one = (np.arange(16)[:, None] == rng.integers(0, 16, (1, L))) & (mode == 1)
            y = np.where(one, x + np.where(x < 128, 1, -1), x)
            a = np.where(mode == 3, np.floor(x * rng.random((16, L))).astype(np.int64), y)
            b = np.where(mode == 2, x + np.floor((255 - x) * rng.random((16, L))).astype(np.int64), y)
            put(lo, hi, e, q, g, c[g, k, np.arange(L)], a, b, np.minimum(np.maximum(rng.integers(-9, 10, (16, L)), -a), 255 - b))
    return pack(lo, hi, e, s, w, d)
def setup_inputs_spread(rng):
    k = (N, 8, 1, W)
    z = np.where(rng.random(k) < 6 * IP, np.exp2(-1 - 9 * rng.random(k)), 0.5)
    lo, hi, e = rules(rng, z, np.floor(np.exp2(8 * rng.random(k))) - 1); s, w, d = start(rng)
    s = np.floor(rng.random((N, 8, 16, L)) * np.exp2(rng.integers(0, 9, (N, 8, 1, L)))).astype(np.int64)
    s = np.where(rng.random((N, 8, 16, L)) < 0.3, 255 - s, s)
    w = np.floor(rng.random((N, 8, 16, 2)) * np.exp2(rng.integers(1, 12, (N, 8, 16, 2)))).astype(np.int64)
    d = np.floor(rng.random((N, 8, 16, ST)) * np.exp2(rng.integers(0, 9, (N, 8, 16, ST)))).astype(np.int64)
    return pack(lo, hi, e, s, w, d)
def check_inputs(d):
    bad = []; v = {k: np.asarray(d[k]).astype(np.float32) for k in ("lo", "hi", "ef", "s0", "dr")}
    for k in v:
        if not np.all(v[k] == np.floor(v[k])): bad.append("whole numbers in " + k)
    if not np.all((v["lo"] >= 0) & (v["lo"] <= v["hi"]) & (v["hi"] <= 255)): bad.append("0 <= lo <= hi <= 255")
    if not np.all((v["lo"] + v["ef"] >= 0) & (v["hi"] + v["ef"] <= 255)): bad.append("lo + ef >= 0 and hi + ef <= 255")
    for k in ("s0", "dr"):
        if not np.all((v[k] >= 0) & (v[k] <= 255)): bad.append("range of " + k)
    if not np.all((d["wt"] >= 0) & (d["wt"] <= 2047)): bad.append("range of wt")
    return bad
def reference(lo, hi, ef, s0, wt, dr):
    tl, th, te, s, d = [x.astype(np.float32).astype(np.int64).reshape(N, 8, 16, -1) for x in (lo, hi, ef, s0, dr)]
    w = wt.astype(np.int64).reshape(N, 8, 16, 2); st = [s[r] for r in range(N)]; y = np.zeros((N, 8, ST, L), np.int64); old = []
    for t in range(ST):
        now = []
        for r in range(N):
            x = st[r]; c = probes(x, w[r]); ix = c.reshape(8, 1, P * L)
            a = np.take_along_axis(tl[r], ix, 2).reshape(8, 16, P, L); b = np.take_along_axis(th[r], ix, 2).reshape(8, 16, P, L)
            ok = np.all((a <= x[:, :, None, :]) & (x[:, :, None, :] <= b), axis=1)
            fired = np.any(ok, axis=1); i = np.argmax(ok, axis=1)
            col = np.take_along_axis(c, i[:, None, :], 1); place = np.take_along_axis(c, np.maximum(i - 1, 0)[:, None, :], 1)[:, 0]
            fl, fh, fe = [np.take_along_axis(v[r], col, 2) for v in (tl, th, te)]
            y[r, :, t] = np.where(fired, i, P)
            st[r] = np.where(fired[:, None, :], x + fe, np.abs(x - d[r, :, :, t:t + 1]))
            now.append((fired, fl, fh, fe, place))
        if t > 0:
            for r in range(N):
                f0, l0, h0, e0, p0 = old[r]; f1, l1, h1, e1, p1 = now[(r + 1) % N]
                cl = np.maximum(l0, l1 - e0); ch = np.minimum(h0, h1 - e0); ce = e0 + e1
                for g in range(8):
                    m = np.flatnonzero(f0[g] & f1[g]); cols, first = np.unique(p0[g][m], return_index=True); k = m[first]
                    tl[r, g][:, cols] = cl[g][:, k]; th[r, g][:, cols] = ch[g][:, k]; te[r, g][:, cols] = ce[g][:, k]
        old = now
        if t < ST - 1: st = [st[(r - 1) % N] for r in range(N)]
    return {"ys": np.stack(st).reshape(N, 128, L).astype(np.float32), "yp": y.reshape(N, 8, ST * L).astype(np.float32)}

from concourse.mybir import AluOpType as A, ActivationFunctionType as F

W, L, P, ST = 4096, 128, 16, 6
WIN = W + 512
MAGIC = 1.5 * 2.0 ** 35

SCRATCH = {"wti": ("sbuf", [128, 8], "int32"), "pi": ("sbuf", [128, 8], "int32"), "pb": ("sbuf", [128, 8], "int32"),
           "wi": ("sbuf", [128, 128], "int32"), "wj": ("sbuf", [128, 128], "int32"),
           "W4": ("sbuf", [128, 32, 16], "float16"), "P16": ("sbuf", [128, 8, 16], "float16"),
           "c18": ("sbuf", [128, 4, 18], "float32"), "cc": ("sbuf", [128, 3, 18], "float32"),
           "RD": ("sbuf", [128, 24, 18], "bfloat16"), "zp": ("sbuf", [128, 8, 16], "float32")}
for _d, _c, _names in (
        ("bfloat16", WIN, "LO HI EF"), ("bfloat16", 4096, "VB"), ("bfloat16", 1536, "HG"), ("bfloat16", 1024, "SR E0 E1"),
        ("bfloat16", 512, "ones ab LS0 LS1 LS2 LS3 LS4 LS5 SB0 SB1 SB2 SB3 SB4 LB1 LB2 LB3 LB4"), ("bfloat16", 288, "ee"),
        ("bfloat16", 144, "fin NK KT"), ("bfloat16", 128, "ID NI M16 Cb half sg tmp CL CH NE L0 LD SS1 SS2 SS3 SS4"),
        ("bfloat16", 8, "drb BO BP"), ("float16", 128, "kc dum CM XM pS rp0 rp1"), ("float32", 768, "YP"), ("float32", 144, "CT PT"),
        ("float32", 128, "l128 kcol colg BM wc Dm zr zt YS"), ("float32", 16, "pf"), ("float32", 8, "wf d2 nd BOf rf"),
        ("uint16", 128, "off"), ("uint16", 8, "ord repF oc ox")):
    for _n in _names.split():
        SCRATCH[_n] = ("sbuf", [128, _c], _d)
for _n in ("PZ", "PX", "PD0", "PD1", "PD2", "PA"):
    SCRATCH[_n] = ("psum", [128, 32, 16], "float32")
for _n in ("PL", "PR"):
    SCRATCH[_n] = ("psum", [128, 512], "float32")

SEMAPHORES = (["cv", "cs", "cp", "cg", "sent", "dlo", "dhi", "def", "dwt", "ds0", "ddr", "dys", "dyp", "dyq"]
              + ["as%d" % t for t in range(ST)] + ["a%s%d" % (x, t) for t in range(1, ST - 1) for x in "lhef"])

PLAN = {
    "v0": [("LO", 0, 4), ("LO", 4, 8), ("LO", 8, 12), ("LO", 12, 16), ("HI", 0, 4), ("HI", 4, 8), ("HI", 8, 10)],
    "s0": [(10, 13), (13, 16)],
    "main0": "v0 v1 v2 v3 g0 v4 g1 r0 v5 r1 v6",
    "pre0": "Z rep zr zp tr off P16 late efd D0 D1 R0 dl",
    "v": [("HI", 0, 4), ("LO", 0, 4), ("LO", 4, 8), ("LO", 8, 12), ("LO", 12, 15), ("LO", 15, 16)],
    "s": [(4, 8), (8, 12), (12, 16)],
    "main": "g0 g1 v0 g2 v1 r0 v2 r1 v3 r2 v4 v5",
    "pre1": "R0 Z sum rep zr zp tr off P16 efd D0 D1 dl D2",
    "pre": "R0 dd XM wx ox Z rep zr zp tr off P16 efd D0 D1 D2 dl CH sh CL sl",
    "tail": "+f snew +s Bhi Blo +lh Bef +e",
}


def rank_program(g, core, T, topo):
    rank = T.rank_of(core)
    if rank is None:
        return
    n = len(T.cores)
    nxt, prv = T.cores[(rank + 1) % n], T.cores[(rank - 1) % n]
    V, S, PE, SY = g.vector, g.scalar, g.tensor, g.sync
    queue = {"v": V, "s": S, "p": PE, "g": g, "y": SY}
    ops, writer, readers = [], {}, {}
    banks = [k for k in SCRATCH if SCRATCH[k][0] == "psum"]

    def op(q, fn, r=(), w=(), sem=None, val=0):
        i = len(ops)
        deps = set()
        for k in r:
            if k in writer:
                deps.add(writer[k])
            if k in banks:
                deps.update(j for j in readers.get(k, []) if ops[j]["q"] != q)
        for k in w:
            if k in writer:
                deps.add(writer[k])
            deps.update(readers.get(k, []))
        if q == "p":
            deps = {j for j in deps if ops[j]["q"] != "p"}
        ops.append({"q": q, "fn": fn, "deps": deps, "sem": sem, "val": val})
        for k in r:
            readers.setdefault(k, []).append(i)
        for k in w:
            writer[k] = i
            readers[k] = []

    def v(fn, r, w): op("v", fn, r, w)
    def mm(out, lhsT, rhs, start, stop, r, w): op("p", lambda: PE.matmul(out, lhsT, rhs, start, stop), r, [w])
    def ts(out, in0, s1, s2, o0, o1, r, w):
        if o1 is None:
            v(lambda: V.tensor_scalar(out, in0, s1, None, o0), r, w)
        else:
            v(lambda: V.tensor_scalar(out, in0, s1, s2, o0, o1), r, w)
    def tt(out, a, b, o, r, w): v(lambda: V.tensor_tensor(out, a, b, o), r, w)
    def cp(out, a, r, w): v(lambda: V.tensor_copy(out, a), r, w)
    def ms(ap, c, w): v(lambda: V.memset(ap, c), [], w)
    def scan(out, a, nk, r, w): v(lambda: V.tensor_tensor_scan(out, a, nk, 0.0, A.add, A.mult), r + ["NK"], w)
    def act(out, a, f, r, w, bias=0.0, scale=1.0): op("s", lambda: S.activation(out, a, f, bias=bias, scale=scale), r, w)
    def iota(ap, pat, w): op("g", lambda: g.iota(ap, pat, 0, 0, allow_small_or_imprecise_dtypes=True), [], w)
    def pick(out, a, pat, cmp_, base, cm, r, w): op("g", lambda: g.affine_select(out, a, pat, cmp_, 0.0, base, cm), r, w)
    def dma(q, out, a, sem, r, w): op(q, lambda: queue[q].dma_start(out, a), r, w, sem=sem, val=16)
    sent = [0]
    def send(dst, out, a, sem, r):
        rid, pid = topo.addr(dst)[:2]
        sent[0] += len(topo.engines(core, dst))
        op("g", lambda: g.remote_dma(out, a, T.sem[sem], T.sem.sent, pid, rid, topo.mask(core, dst)), r, [], sem="remote")
    def arrives(src, sem, w): op("x", None, [], w, sem=sem, val=len(topo.engines(src, core)))
    def win(name): return T[name][:, 0:WIN]
    def fin(q): return 72 * (q % 2) + 18 * (q // 2) + 17

    dma("y", T.LS0[:, 0:128], T.s0[:], "ds0", [], ["LS0"])
    dma("s", T.wti[:, 0:2], T.wt[:], "dwt", [], ["wti"])
    dma("y", T.LO[:, 0:W], T.lo[:], "dlo", [], ["LO"])
    dma("s", T.drb[:, 0:ST], T.dr[:], "ddr", [], ["drb"])
    dma("y", T.HI[:, 0:W], T.hi[:], "dhi", ["LS0"], ["HI"])
    dma("y", T.EF[:, 0:W], T.ef[:], "def", ["LO"], ["EF"])
    arrives(prv, "as0", ["L0"])
    arrives(prv, "as1", ["LD"])
    for t in range(2, ST):
        arrives(prv, "as%d" % t, ["LS%d" % t])
    for t in range(1, ST - 1):
        for w_ in PLAN["tail"].split():
            if w_[0] == "+" and w_ != "+s":
                arrives(nxt, "a%s%d" % (w_[1], t), ["LB%d%s" % (t, x) for x in w_[1:]])

    pi = T.pi[:, 0:1]
    op("g", lambda: g.iota(pi, [[0, 1]], 0, 1), [], ["pi"])
    iota(T.colg[:], [[1, 2], [2, 4], [0, 16]], ["colg"])
    iota(T.kcol[:], [[0, 8], [1, 16]], ["kcol"])
    iota(T.l128[:], [[1, 128]], ["l128"])
    ms(T.ones[:], 1.0, ["ones"])
    ms(T.W4[:], 0.0, ["W4"])
    ms(T.half[0:32, :], 0.5, ["half"])
    ms(T.cc[:, 0, :], 0.0, ["cc1"])
    for x in ("LO", "HI", "EF"):
        act(T[x][:, W:WIN], T.ones[:], F.Copy, ["ones"], [x + "t"])
    ts(T.pb[:, 0:1], pi, 4, None, A.logical_shift_right, None, ["pi"], ["pb0"])
    ts(T.pb[:, 1:2], pi, 15, None, A.bitwise_and, None, ["pi"], ["pb1"])
    ts(T.pb[:, 2:3], pi, 3, None, A.bitwise_and, None, ["pi"], ["pb2"])
    ts(T.pb[:, 3:4], pi, 2, 1, A.logical_shift_right, A.bitwise_and, ["pi"], ["pb3"])
    ts(T.pb[:, 4:5], pi, 3, 1, A.logical_shift_right, A.bitwise_and, ["pi"], ["pb4"])
    cp(T.pf[:, 5:6], pi, ["pi"], ["pf5"])
    cp(T.pf[:, 0:5], T.pb[:, 0:5], ["pb0", "pb1", "pb2", "pb3", "pb4"], ["pf"])
    ts(T.pf[:, 8:9], T.pf[:, 5:6], 256.0, 2048.0, A.mult, A.add, ["pf5"], ["pf8"])
    ts(T.BM[:], T.colg[:], T.pf[:, 0:1], None, A.is_equal, None, ["colg", "pf"], ["BM"])
    ts(T.pf[:, 6:7], T.pf[:, 2:3], 32.0, T.pf[:, 4:5], A.mult, A.add, ["pf"], ["pf6"])
    ts(T.kc[0:32, :], T.kcol[0:32, :], -2048.0, None, A.add, None, ["kcol"], ["kc"])
    ts(T.pf[:, 7:8], T.pf[:, 3:4], 16.0, T.pf[:, 6:7], A.mult, A.add, ["pf", "pf6"], ["pf7"])
    ts(T.c18[:, 0, :], T.l128[:, 0:18], T.pf[:, 1:2], None, A.add, None, ["l128", "pf"], ["c0"])
    ts(T.ord[:], T.l128[:, 0:8], 2.0, T.pf[:, 7:8], A.mult, A.add, ["l128", "pf7"], ["ord"])
    ts(T.BOf[:], T.l128[:, 0:8], T.pf[:, 0:1], None, A.is_equal, None, ["l128", "pf"], ["BOf"])
    ts(T.wf[:, 0:1], T.wti[:, 0:1], 2048.0, None, A.add, None, ["wti"], ["wf0"])
    ts(T.wf[:, 1:2], T.wti[:, 1:2], 2.0, None, A.mult, None, ["wti"], ["wf1"])
    ts(T.c18[:, 1, :], T.c18[:, 0, :], 17.0, None, A.is_equal, None, ["c0"], ["c1"])
    ts(T.wi[:], T.kcol[:], T.wf[:, 1:2], T.wf[:, 0:1], A.mult, A.add, ["kcol", "wf0", "wf1"], ["wi"])
    ts(T.c18[:, 2, :], T.c18[:, 0, :], 16.0, None, A.is_equal, None, ["c0"], ["c2"])
    ts(T.wj[:], T.wi[:], W - 1, None, A.bitwise_and, None, ["wi"], ["wj"])
    tt(T.cc[:, 1, :], T.c18[:, 1, :], T.c18[:, 2, :], A.subtract, ["c1", "c2"], ["cc0"])
    ts(T.wc[:], T.wj[:], -2048.0, None, A.add, None, ["wj"], ["wc"])
    ts(T.ID[:], T.l128[:], T.pf[:, 5:6], None, A.is_equal, None, ["l128", "pf5"], ["ID"])
    tt(T.W4[:, 0:16:2, :], T.wc[:], T.BM[:], A.mult, ["wc", "BM", "W4"], ["W4a"])
    tt(T.W4[:, 17:32:2, :], T.wc[:], T.BM[:], A.mult, ["wc", "BM", "W4"], ["W4b"])
    cp(T.BO[:], T.BOf[:], ["BOf"], ["BO"])
    cp(T.BP[:], T.BM[:, 0:128:16], ["BM"], ["BP"])
    pick(T.fin[0:2, :], T.ones[0:2, 0:144], [[0, 8], [1, 18]], A.is_equal, -17, 0, ["ones"], ["fin"])
    iota(T.rf[:], [[18, 4], [72, 2]], ["rf"])
    pick(T.ee[0:2, 0:144], T.ones[0:2, 0:144], [[-100, 2], [0, 4], [1, 18]], A.is_equal, 99, -100, ["ones"], ["ee0"])
    pick(T.ee[0:2, 144:288], T.ones[0:2, 0:144], [[100, 2], [0, 4], [1, 18]], A.is_equal, -1, -100, ["ones"], ["ee1"])
    send(nxt, T.L0[:], T.LS0[:, 0:128], "as0", ["LS0"])
    pick(T.SR[0:8, 0:512], T.ones[0:8, :], [[1, 4], [0, 128]], A.is_equal, 0, -1, ["ones"], ["SR0"])
    pick(T.SR[0:8, 512:1024], T.ones[0:8, :], [[1, 4], [0, 128]], A.is_equal, 4, -1, ["ones"], ["SR1"])
    RDK = ["RD%d%d" % (y, G) for y in range(2) for G in range(4)]

    def later_constants():
        ts(T.dum[0:32, :], T.l128[0:32, :], 2.0, T.pf[0:32, 8:9], A.mult, A.add, ["l128", "pf8"], ["dum"])
        ts(T.M16[:], T.kcol[:], T.pf[:, 1:2], None, A.is_equal, None, ["kcol", "pf"], ["M16"])
        ts(T.cc[:, 0, 1:2], T.cc[:, 1, 2:3], 0.0, None, A.min, None, ["cc0", "cc1"], ["ccb"])
        ts(T.repF[:], T.rf[:], 17.0, None, A.add, None, ["rf"], ["repF"])
        act(T.d2[:, 0:ST], T.drb[:, 0:ST], F.Identity, ["drb"], ["d2"], scale=2.0)
        act(T.nd[:, 0:ST], T.drb[:, 0:ST], F.Identity, ["drb"], ["nd"], scale=-1.0)
        act(T.cc[:, 0, 2:16], T.cc[:, 1, 3:17], F.Copy, ["cc0", "cc1"], ["cca"])
        act(T.cc[:, 0, 17:18], T.cc[:, 1, 17:18], F.Copy, ["cc0", "cc1"], ["ccc"])
        act(T.cc[:, 2, :], T.cc[:, 0, :], F.Copy, ["cca", "ccb", "ccc"], ["ccd"])
        for y in range(2):
            for G in range(4):
                act(T.RD[:, y * 12 + G:y * 12 + 12:4, :], T.cc[:], F.Identity, ["cc0", "ccd", "BOf"], ["RD%d%d" % (y, G)],
                    scale=T.BOf[:, 2 * G + y:2 * G + y + 1])
        act(T.NI[:], T.ID[:], F.Identity, ["ID"], ["NI"], scale=-1.0)
        act(T.pf[:, 9:10], T.pf[:, 5:6], F.Identity, ["pf5"], ["pf9"], bias=2304.0, scale=2.0)
        act(T.Cb[:], T.M16[:], F.Identity, ["M16"], ["Cb"], bias=16384.0, scale=-8192.0)
        act(T.Dm[:], T.M16[:], F.Identity, ["M16", "pf9"], ["Dm"], scale=T.pf[:, 9:10])

    def z_const():
        mm(T.PZ[:, 0:8, :], T.kc[0:1, :], T.ones[0:1, 0:128], True, False, ["kc", "ones"], "PZ")
        mm(T.PZ[:, 0:8, :], T.half[0:1, :], T.ones[0:1, 0:128], False, False, ["half", "ones"], "PZ")

    def z_sum(src, key, stop):
        for y in range(2):
            for b in range(2):
                mm(T.PZ[:, b:8:2, :], T.W4[:, y * 16 + 8 * b:y * 16 + 8 * b + 8, :], src[:, 64 * y:64 * y + 64], False,
                   stop and y + b == 2, ["W4a", "W4b", key], "PZ")

    def step(t):
        LS, ls, lr = T["LS%d" % t], "LS%d" % t, "LR%d" % t
        st = LS[:, 0:128]
        comp = t >= 2
        back = 1 <= t <= ST - 2
        keep = t <= ST - 3
        vl, sl, pl = [PLAN[x + ("0" if t == 0 else "")] for x in ("v", "s", "main")]
        lb, sa, e = "LB%d" % (t - 1), "SB%d" % (t - 2), "E%d" % (t % 2)
        ox = T.ox[:, 0:8]

        def pre(w_):
            if w_ == "Z":
                if t == 1:
                    z_sum(T.LD, "LD", True)
                else:
                    z_sum(LS, ls, True)
            elif w_ == "sum":
                tt(st, T.L0[:], T.LD[:], A.add, ["L0", "LD"], [ls])
            elif w_ == "rep":
                act(LS[:, 128:256], st, F.Copy, [ls], [lr + "a"])
                act(LS[:, 256:512], LS[:, 0:256], F.Copy, [ls, lr + "a"], [lr])
            elif w_ == "zr":
                ts(T.zr[:], T.PZ[:, 0:8, :], MAGIC, MAGIC, A.add, A.subtract, ["PZ"], ["zr"])
            elif w_ == "zp":
                tt(T.zp[:], T.PZ[:, 0:8, :], T.zr[:], A.subtract, ["PZ", "zr"], ["zp"])
            elif w_ == "tr":
                v(lambda: V.transpose(T.zt[:], T.zp[:]), ["zp"], ["zt"])
            elif w_ == "off":
                ts(T.off[:], T.zt[:, 0:128].indirect(T.ord[:, 0:8]), 2047.5, None, A.add, None, ["zt", "ord"], ["off"])
            elif w_ == "P16":
                for b in range(2):
                    ts(T.P16[:, 4 * b:4 * b + 4, :], T.zp[:, b:8:2, :], -0.5, None, A.add, None, ["zp"], ["P16%d" % b])
            elif w_ == "late":
                later_constants()
            elif w_ == "efd":
                act(T.tmp[:], st, F.Relu, [ls, "d2"], ["tmp"], bias=T.d2[:, t:t + 1], scale=-2.0)
                act(T.EF[:, W:W + 256:2], T.tmp[:], F.Identity, ["tmp", "nd"], ["EFt"], bias=T.nd[:, t:t + 1])
            elif w_ == "dd":
                mm(T.PX[:, 0:8, :], T.NI[:], T[lb][:, 384:512], False, False, ["NI", lb + "f"], "PX")
                for q in range(8):
                    mm(T.PX[:, q, :], T[e][:, 128 * q:128 * q + 128], T[lb][:, 384 + 16 * q:400 + 16 * q], False, q == 7,
                       [e, lb + "f"], "PX")
            elif w_ == "CH":
                tt(T.CH[:], T.PA[:, 8:16, :], T[lb][:, 128:256], A.min, ["PA", lb + "h"], ["CH"])
            elif w_ == "CL":
                tt(T.CL[:], T.PA[:, 0:8, :], T[lb][:, 0:128], A.max, ["PA", lb + "l"], ["CL"])
            elif w_ == "XM":
                tt(T.XM[:], T.PX[:, 0:8, :], T.Dm[:], A.min, ["PX", "Dm"], ["XM"])
            elif w_ == "wx":
                mm(T.PX[:, 8, 0:8], T.XM[:], T.BO[:], True, True, ["XM", "BO"], "PX")
            elif w_ == "ox":
                ts(T.ox[:], T.PX[:, 8, 0:8], 2048.0, None, A.add, None, ["PX"], ["ox"])
            elif w_ == "sh":
                tt(win("HI").indirect(ox), T.CH[:], T.NE[:], A.add, ["CH", "NE", "ox"], ["HI", "HIt"])
            elif w_ == "sl":
                tt(win("LO").indirect(ox), T.CL[:], T.NE[:], A.add, ["CL", "NE", "ox"], ["LO", "LOt"])
            elif w_ == "se":
                tt(win("EF").indirect(ox), T[sa][:, 256:384], T[lb][:, 256:384], A.add, [sa + "e", lb + "e", "ox"], ["EF", "EFt"])
            elif w_ == "R0":
                mm(T.PR[:, 0:144], T.ones[0:1, 0:128], T.fin[0:1, :], True, False, ["ones", "fin"], "PR")
            elif w_ == "dl":
                mm(T.PL[:, 0:288], T.dum[0:2, :], T.ee[0:2, :], True, False, ["dum", "ee0", "ee1"], "PL")
                for y in range(2):
                    for b in range(2):
                        mm(T.PL[64 * y:64 * y + 64, 144 * b:144 * b + 144], T.P16[:, 4 * b:4 * b + 4, :],
                           T.RD[:, 12 * y + 4 * b:12 * y + 4 * b + 8, :], False, b == 1, ["P160", "P161"] + RDK, "PL")
            else:
                i = int(w_[1])
                c = 128 * (sl[i][1] - sl[i][0])
                mm(T["P" + w_][:, 0:c // 16, :], T.ID[:], LS[:, 0:c], True, False, ["ID", ls, lr], "P" + w_)

        for w_ in PLAN["pre" + ("" if comp else str(t))].split():
            pre(w_)
        pl = pl.split()
        for w_ in pl:
            i = int(w_[1])
            name, k0, k1 = vl[i] if w_[0] == "v" else ("HI",) + tuple(sl[i])
            c0, c, pd = (0 if name == "LO" else 2048) + 128 * k0, 128 * (k1 - k0), "PD%d" % i
            picked = win(name).indirect(T.off[:, 8 * k0:8 * k1])
            if w_[0] == "g":
                act(T.HG[:, 512 * i:512 * i + c], picked, F.Identity, ["HI", "HIt", "off"], ["HG%d" % i], scale=-1.0)
                mm(T[pd][:, 0:c // 16, :], T.ID[:], T.HG[:, 512 * i:512 * i + c], False, True, ["ID", "HG%d" % i], pd)
                continue
            if w_[0] == "v":
                tt(T.VB[:, c0:c0 + c], picked, LS[:, 0:c], A.is_gt if name == "LO" else A.is_lt,
                   [name, name + "t", "off", ls, lr], ["V" + w_])
            else:
                act(T.VB[:, c0:c0 + c], T[pd][:, 0:c // 16, :], F.Relu, [pd], ["V" + w_])
            for k in range(k0, k1):
                mm(T.PR[:, 16 - k:144:18], T.VB[:, c0 + 128 * (k - k0):c0 + 128 * (k - k0 + 1)], T.BP[:], False,
                   w_ == pl[-1] and k == k1 - 1, ["V" + w_, "BP"], "PR")
        if comp:
            pre("se")
        sb, s0, ss = "SB%d" % t, "SB%d" % (t - 1), "SS%d" % t
        if t < ST - 1:
            z_const()
        if t == 0:
            z_sum(T.L0, "L0", False)
        if back:
            mm(T.PA[:, 0:8, :], T.ID[:], T[s0][:, 0:128], True, False, ["ID", s0 + "l"], "PA")
            mm(T.PA[:, 0:8, :], T.ID[:], T[s0][:, 256:384], False, True, ["ID", s0 + "e"], "PA")
        if comp:
            act(T.NK[:], T.PR[:, 0:144], F.Sign, ["PR"], ["NK"])
        else:
            ts(T.NK[:], T.PR[:, 0:144], 1.0, None, A.min, None, ["PR"], ["NK"])
        scan(T.CT[:], T.PL[:, 72:216], T.NK[:], ["PL"], ["CT"])
        tt(T.CM[:], T.CT[:, 0:144].indirect(T.repF[:, 0:8]), T.M16[:], A.mult, ["CT", "repF", "M16"], ["CM"])
        if back:
            act(T.sg[:], T.CT[:, 0:144].indirect(T.repF[:, 0:8]), F.Sign, ["CT", "repF"], ["sg"], bias=2047.5, scale=-1.0)
            act(T[sb][:, 384:512], T.sg[:], F.Identity, ["sg"], [sb + "f"], bias=4096.0, scale=4096.0)
        mm(T.PX[:, 8, 0:8], T.CM[:], T.BO[:], True, True, ["CM", "BO"], "PX")
        scan(T.KT[:], T.ones[:, 0:144], T.NK[:], ["ones"], ["KT"])
        ts(T.oc[:], T.PX[:, 8, 0:8], 2048.0, None, A.add, None, ["PX"], ["oc"])
        oc = T.oc[:, 0:8]

        def kout():
            mm(T.PD2[0:8, 0:8, :], T.KT[:, 16:144:18], T.ID[:], True, True, ["KT", "ID"], "PD2")
            act(T.YP[0:8, 128 * t:128 * t + 128], T.PD2[0:8, 0:8, :], F.Copy, ["PD2"], ["YP%d" % t])
        if t == ST - 1:
            kout()
            dma("s", T.yp[0:8:2, :], T.YP[0:4, :], "dyp", ["YP%d" % u for u in range(ST)], ["yp"])
            dma("s", T.yp[1:8:2, :], T.YP[4:8, :], "dyq", ["YP%d" % u for u in range(ST)], ["yq"])
            tt(T.YS[:], win("EF").indirect(oc), st, A.add, ["EF", "EFt", "oc", ls], ["YS"])
            dma("y", T.ys[:], T.YS[:], "dys", ["YS"], ["ys"])
            return
        for w_ in (PLAN["tail"] if back else "Vef +d Bhi Blo").split():
            if w_ == "Blo":
                cp(T[sb][:, 0:128], win("LO").indirect(oc), ["LO", "LOt", "oc"], [sb + "l"])
            elif w_ == "Bhi":
                act(T[sb][:, 128:256], win("HI").indirect(oc), F.Identity, ["HI", "HIt", "oc"], [sb + "h"])
            elif w_ == "Bef":
                act(T[sb][:, 256:384], win("EF").indirect(oc), F.Identity, ["EF", "EFt", "oc"], [sb + "e"])
            elif w_ == "Vef":
                cp(T[sb][:, 256:384], win("EF").indirect(oc), ["EF", "EFt", "oc"], [sb + "e"])
            elif w_ == "snew":
                tt(T[ss][:], win("EF").indirect(oc), st, A.add, ["EF", "EFt", "oc", ls], [ss])
            elif w_ == "+d":
                send(nxt, T.LD[:], T[sb][:, 256:384], "as1", [sb + "e"])
            elif w_ == "+s":
                send(nxt, T["LS%d" % (t + 1)][:, 0:128], T[ss][:], "as%d" % (t + 1), [ss])
            else:
                a, b = 128 * "lhef".index(w_[1]), 128 * "lhef".index(w_[-1]) + 128
                send(prv, T["LB%d" % t][:, a:b], T[sb][:, a:b], "a%s%d" % (w_[1], t), [sb + x for x in w_[1:]])
        if back:
            mm(T.PA[:, 8:16, :], T.ID[:], T[s0][:, 128:256], True, False, ["ID", s0 + "h"], "PA")
            mm(T.PA[:, 8:16, :], T.ID[:], T[s0][:, 256:384], False, True, ["ID", s0 + "e"], "PA")
            r0 = "rp%d" % ((t - 1) % 2)
            mm(T.PX[:, 0:8, :], T.ID[:], T[r0][:], True, False, ["ID", r0], "PX")
            mm(T.PX[:, 0:8, :], T.ID[:], T.Cb[:], False, False, ["ID", "Cb"], "PX")
            act(T.NE[:], T[s0][:, 256:384], F.Identity, [s0 + "e"], ["NE"], scale=-1.0)
        rp, E = "rp%d" % (t % 2), T[e]
        if keep:
            scan(T.PT[:, 0:72], T.PL[:, 0:72], T.NK[:, 0:72], ["PL"], ["PT"])
            scan(T.PT[:, 72:144], T.PL[:, 216:288], T.NK[:, 72:144], ["PL"], ["PU"])
            cp(T[rp][:], T.PT[:, 0:144].indirect(T.repF[:, 0:8]), ["PT", "PU", "repF"], [rp])
            mm(T.PR[0:8, 0:128], T[rp][:, 0:128:16], T.ID[:], True, True, [rp, "ID"], "PR")
        kout()
        if keep:
            cp(T.pS[0:8, :], T.PR[0:8, 0:128], ["PR"], ["pS"])
            for q in (4, 5, 6, 7, 0, 1, 2, 3):
                mm(T["PD%d" % (q // 4)][:, 8 * (q % 4):8 * (q % 4) + 8, :], T.SR[0:8, 128 * q:128 * q + 128], T.pS[0:8, :],
                   True, True, ["SR0", "SR1", "pS"], "PD%d" % (q // 4))
            for q in range(4, 8):
                act(T.ab[:, 128 * (q - 4):128 * (q - 3)], T.PD1[:, 8 * (q - 4):8 * (q - 3), :], F.Abs, ["PD1", "PT", "PU"],
                    ["ab%d" % q], bias=T.PT[:, fin(q):fin(q) + 1], scale=-1.0)
            for q in range(4):
                ts(E[:, 128 * q:128 * q + 128], T.PD0[:, 8 * q:8 * q + 8, :], T.PT[:, fin(q):fin(q) + 1], None, A.is_equal,
                   None, ["PD0", "PT", "PU", e], [e + str(q)])
            act(E[:, 512:1024], T.ab[:], F.Relu, ["ab4", "ab5", "ab6", "ab7", e], [e + "s"], bias=1.0, scale=-1.0)
            pick(E[:], E[:], [[0, 8], [1, 128]], A.is_gt, 0, -1, [e + x for x in "0123s"], [e])

    z_const()
    for t in range(ST):
        step(t)
    op("g", None, ["ys", "yp", "yq"], [])

    seen = {q: {} for q in queue}
    need = set()
    for o in ops:
        o["waits"] = []
        if o["q"] == "x":
            continue
        top = {}
        for j in o["deps"]:
            key = ops[j]["sem"] or ops[j]["q"]
            top[key] = max(top.get(key, -1), j)
        for key in sorted(top):
            if seen[o["q"]].get(key, -1) < top[key]:
                seen[o["q"]][key] = top[key]
                o["waits"].append(top[key])
                need.add(top[key])
    count = {q: 0 for q in queue}
    for i, o in enumerate(ops):
        if o["sem"] is None and i in need:
            count[o["q"]] += 1
            o["sig"] = ("c" + o["q"], count[o["q"]], 1)
        elif o["sem"] not in (None, "remote"):
            o["sig"] = (o["sem"], o["val"], o["val"])
        if o["q"] == "x":
            continue
        for j in o["waits"]:
            queue[o["q"]].wait_ge(T.sem[ops[j]["sig"][0]], ops[j]["sig"][1])
        if o["fn"] is not None:
            ins = o["fn"]()
            if "sig" in o:
                ins.then_inc(T.sem[o["sig"][0]], o["sig"][2])
    g.wait_ge(T.sem.sent, sent[0])
